import numpy as np, ml_dtypes
CORES = [40,41,42,43,44,45,46,47]
N = 8
BF = ml_dtypes.bfloat16
def gentries(a):
    return np.ascontiguousarray(a.reshape(8, 16, -1).transpose(0, 2, 1)).reshape(8, -1)
def gtable(e):
    e = np.asarray(e); return np.ascontiguousarray(e.reshape(8, -1, 16).transpose(0, 2, 1)).reshape(128, -1).astype(np.int32)
W, K, L, T = 4608, 1024, 1, 2
TOP, NEG, EMPTY = 255, 9, 16
def parts(rng):
    j = rng.integers(0, W, (N, 8, 16, W), dtype=np.int32)
    x = rng.integers(0, 16, (N, 8, N, L, K)); x = np.where(rng.random(x.shape) < 0.125, EMPTY, x)
    return j, x, rng.integers(0, 16, (N, 8, K)), rng.integers(0, W, (N, 8, T, K))
def coef(rng, drift):
    c = drift + 50.0 * rng.standard_normal((N, 8, 1, W), dtype=np.float32) + 40.0 * rng.standard_normal((N, 8, 16, W), dtype=np.float32)
    return np.minimum(np.maximum(np.rint(c), -128), 127)
def pack(j, c, x, y, a):
    return {"jm": np.ascontiguousarray(j.reshape(N, 128, W)).astype(np.int32), "cf": (np.ascontiguousarray(c.reshape(N, 128, W)).astype(np.float32) + 0.0).astype(BF),
            "lt": np.ascontiguousarray(x.reshape(N, 8, N * L * K)).astype(np.float32).astype(BF), "y0": np.ascontiguousarray(y).astype(np.float32).astype(BF),
            "st": np.stack([gtable(q.reshape(8, T * K)) for q in a])}
def setup_inputs(rng):
    j, x, y, a = parts(rng)
    return pack(j, coef(rng, rng.choice(np.array([5.0, 15.0, 30.0, 45.0]), (N, 8, 1, 1))), x, y, a)
def setup_inputs_ties(rng):
    j, x, y, a = parts(rng); n = rng.choice(np.array([4, 6, 7, 8, 9]), (N, 8, 1, W))
    o = np.argsort(rng.random((N, 8, 16, W)), axis=2); c = np.where(o < n, -1, (rng.random(o.shape) < 0.8).astype(np.int64))
    p = rng.permutation(16)[:, None]
    c[:, 0] = np.where(p < 8, -1, 1); c[:, 1] = np.where(p < 9, -1, 1); c[:, 2] = np.where(p < 8, -1, 0)
    return pack(j, c, x, y, a)
def setup_inputs_clip(rng):
    j, x, y, a = parts(rng); s = np.where(rng.random((N, 8, 1, W)) < 0.75, 1, -1)
    c = s * rng.integers(100, 128, (N, 8, 16, W)); c = np.where(rng.random(c.shape) < 0.1, -c, c)
    c[:, 1::2, :5] = -np.abs(c[:, 1::2, :5]) - 1
    r = int(rng.integers(0, N)); x[:, 6, r] = rng.integers(0, 16, (N, L, K)); e = 127 // L
    for d in range(N):
        q = (r + d) % N; c[q, 6] = 1; c[q, 6, 1:8] = -1
        c[q, 6, 8] = -1 if d == 3 else 0
        c[q, 6, 0] = (-128, e, e, 255 - 2 * L * e)[d] if d < 4 else 0
    return pack(j, c, x, y, a)
def setup_inputs_gaps(rng):
    j, x, y, a = parts(rng); x = np.where(rng.random(x.shape) < 0.5, EMPTY, x)
    x[:, 0] = EMPTY; x[:, 1:4] = rng.integers(0, 16, (N, 3, N, L, K))
    for q in range(N):
        for s in range(N):
            if q != s: x[q, 2, s] = EMPTY
            if q != (s - 1) % N: x[q, 3, s] = EMPTY
    c = coef(rng, 20.0); r = int(rng.integers(0, N))
    c[r, 0] = -rng.integers(1, 129, (16, W)); c[r, 1] = -128; c[r, 1, 8:] += (rng.random(W) < 0.5).astype(np.float32)
    x[r, 1, r, 1:] = EMPTY
    return pack(j, c, x, y, a)
def setup_inputs_alike(rng):
    j, x, y, a = parts(rng)
    j[:, ::2] = rng.choice(np.array([0, W - 1, W // 2, 5], np.int32), (N, 4, 16, W)); j[:, 1] = np.arange(W)
    j[:, 6] = rng.integers(0, W, (N, 1, 1))
    x[:, 3] = rng.integers(0, 16, (N, 1, 1, 1)); y[:, 3] = rng.integers(0, 16, (N, 1))
    a[:, 2] = rng.integers(0, W, (N, 1, 1)); a[:, 5] = rng.choice(np.array([0, W - 1]), (N, T, K))
    c = coef(rng, 25.0); r = int(rng.integers(0, N)); c[r] = np.minimum(np.abs(c[r]), 127)
    return pack(j, c, x, y, a)
def setup_inputs_spread(rng):
    j, x, y, a = parts(rng)
    j = np.minimum((W * rng.random(j.shape) ** 3).astype(np.int64), W - 1); a = np.minimum((W * rng.random(a.shape) ** 3).astype(np.int64), W - 1)
    c = np.exp2(8.0 * rng.random((N, 8, 1, W))) * (0.5 * rng.standard_normal((N, 8, 16, W)) + 0.25)
    x = np.minimum((17 * rng.random(x.shape) ** 2).astype(np.int64), EMPTY); y = np.minimum((16 * rng.random(y.shape) ** 2).astype(np.int64), 15)
    return pack(j, np.minimum(np.maximum(np.rint(c), -128), 127), x, y, a)
def check_inputs(d):
    bad = []
    for k, lo, hi in (("jm", 0, W - 1), ("cf", -128, 127), ("lt", 0, 16), ("y0", 0, 15), ("st", 0, W - 1)):
        a = np.asarray(d[k]).astype(np.float32)
        if not (np.all(a == np.floor(a)) and np.min(a) >= lo and np.max(a) <= hi): bad.append("range of " + k)
        if np.any(np.signbit(a) & (a == 0)): bad.append("-0.0 in " + k)
    return bad
def reference(jm, cf, lt, y0, st):
    J = jm.astype(np.int64).reshape(N, 8, 16, W); C = cf.astype(np.float32).astype(np.int64).reshape(N, 8, 16, W)
    x = lt.astype(np.float32).astype(np.int64).reshape(N, 8, N, L, K); y = y0.astype(np.float32).astype(np.int64)
    start = np.stack([gentries(a) for a in st]).astype(np.int64).reshape(N, 8, T, K)
    new = np.full((N, 8, T, K), EMPTY, np.int64); v = np.zeros((N, 8, 16, K), np.int64); g = np.arange(8)[:, None]
    for t in range(T):
        for s in range(N):
            b = J[s][g, y[s], start[s, :, t]]; u = np.take_along_axis(C[s], b[:, None, :], 2)
            live = np.ones((8, K), bool)
            for d in range(N):
                q = (s + d) % N
                slots = [new[s, :, i] for i in range(t - 1, -1, -1)] if d == 0 else []
                for z in slots + [x[q, :, s, l] for l in range(L)]:
                    go = live & (z < EMPTY)
                    b = np.where(go, J[q][g, np.minimum(z, 15), b], b)
                    w = np.minimum(np.maximum(u + np.take_along_axis(C[q], b[:, None, :], 2), -TOP), TOP)
                    u = np.where(go[:, None, :], w, u)
                    hit = go & (np.add.reduce((u < 0).astype(np.int64), axis=1) >= NEG)
                    z[hit] = EMPTY; live = live & ~hit
            new[s, :, t] = np.where(live, y[s], EMPTY)
            y[s] = np.argmax(u, axis=1)
            v[s] = u
    return {"yl": x.reshape(N, 8, N * L * K).astype(np.float32).astype(BF), "yi": new.reshape(N, 8, T * K).astype(np.float32).astype(BF), "yv": v.reshape(N, 128, K).astype(np.float32).astype(BF)}

@@ -1,0 +1,666 @@
+import math
+from concourse.mybir import AluOpType, ActivationFunctionType
+
+ALU, AF = AluOpType, ActivationFunctionType
+N, W, NK = 8, 4608, 1024
+NCH = 2
+n = NK // NCH
+K = n // 16
+NH = 2
+h = n // NH
+PLAN = [[2, 2, 2, 2], [2, 2, 2, 2]]
+NT = max(max(p) for p in PLAN)
+CWID = W + 32
+PER = 72.0
+SC = math.log(2.0) / PER
+A = PER / math.log(2.0)
+HIT = -22.25
+STOP = 44.5
+JB = 6
+JBW = W // JB
+B16, F32, I32, U16 = "bfloat16", "float32", "int32", "uint16"
+
+ST = []
+for _w in range(2):
+    _o, _l = 0, []
+    for _m in PLAN[_w]:
+        _l.append((_o, _m))
+        _o += _m
+    ST.append(_l)
+
+
+def nslots(w, i):
+    return ST[w][i][1] + (1 if w == 1 and i == 0 else 0)
+
+
+SCRATCH, SEMAPHORES = {}, ["kpe", "kv", "ks", "kg", "ls", "lcf", "lst", "llt", "ly", "stores"]
+PLACE = {}
+
+
+def sb(name, cols, dtype=B16):
+    SCRATCH[name] = ("sbuf", [128, cols], dtype)
+    PLACE[name] = (name, 0)
+
+
+def tile(kind, key, cols, dtype=B16):
+    buf = "z" + kind
+    at = SCRATCH[buf][1][1] if buf in SCRATCH else 0
+    SCRATCH[buf] = ("sbuf", [128, at + cols], dtype)
+    PLACE[kind + key] = (buf, at)
+
+
+sb("JW", (1 + NT) * W)
+sb("CW", NT * CWID)
+sb("jmi", W, I32)
+sb("jmf", W, F32)
+sb("io5", 576, F32)
+for _k in ("ones", "RM", "SM", "AM"):
+    sb(_k, 2048)
+for _k in ("ID", "I4", "I8", "LTa", "LTb", "LTR"):
+    sb(_k, 128)
+sb("b8a", 8)
+sb("b8", 8)
+sb("ipi", 2, I32)
+sb("ipj", 2, I32)
+sb("ipf", 2, F32)
+sb("sti", 128, I32)
+sb("stu", 128, U16)
+for _k in ("y0l", "y1l", "yim"):
+    sb(_k, 64)
+sb("yit", 128)
+for _k in ("ohn", "ohy", "ohr"):
+    sb(_k, NK)
+SEMAPHORES += ["ljm%d" % _b for _b in range(JB)]
+for _e in range(NT):
+    sb("lt%d" % _e, 512)
+for _c in range(NCH):
+    for _k in ("mj", "sg", "cc", "vb", "ax"):
+        sb("%s%d" % (_k, _c), n)
+    sb("am%d" % _c, 2 * n)
+    sb("tt%d" % _c, K, F32)
+    sb("ta%d" % _c, 3 * K, F32)
+    sb("jl%d" % _c, K, U16)
+    sb("cl%d" % _c, K, U16)
+    for _k in ["ps", "w"] + ["pv%d" % _x for _x in range(NH)]:
+        SCRATCH["%s%d" % (_k, _c)] = ("psum", [128, 512], F32)
+        PLACE["%s%d" % (_k, _c)] = ("%s%d" % (_k, _c), 0)
+OHS = []
+for _w in range(2):
+    for _o, _m in ST[_w]:
+        for _e in range(_m):
+            if (_o, _e) not in OHS:
+                OHS.append((_o, _e))
+sb("oh", NK * len(OHS))
+MOVES = []
+for _i, (_o, _m) in enumerate(ST[0]):
+    for _k, (_p, _q) in enumerate(ST[1]):
+        _lo, _hi = max(_o, _p), min(_o + _m, _p + _q)
+        if _o != _p and _lo < _hi:
+            MOVES.append((_i, _k, _lo, _hi))
+            tile("mv", "%d%d" % (_i, _k), 64 * (_hi - _lo))
+            SEMAPHORES.append("rmv%d%d" % (_i, _k))
+for _w in range(2):
+    for _i, (_o, _m) in enumerate(ST[_w]):
+        _s = nslots(_w, _i)
+        _x = "%d%d" % (_w, _i)
+        tile("dd", _x, 64 * (_s + 1))
+        tile("es", _x, 64 * _s)
+        tile("ej", _x, 64 * _s, F32)
+        tile("hi", _x, 64 * _s)
+        tile("ls", _x, 64 * _m)
+        tile("do", _x, 64)
+        tile("di", _x, 64)
+        for _c in range(NCH):
+            _y = "%s%d" % (_x, _c)
+            tile("vo", _y, n)
+            tile("vi", _y, n)
+            SEMAPHORES += ["rv" + _y, "rd" + _y]
+            if _i + 1 < len(ST[_w]):
+                tile("to", _y, K, F32)
+                tile("ti", _y, K, F32)
+                SEMAPHORES.append("rt" + _y)
+for _i, (_o, _m) in enumerate(ST[1]):
+    for _e in range(1, _m):
+        tile("yr", "%d%d" % (_i, _e), 64)
+        SEMAPHORES.append("ry%d%d" % (_i, _e))
+for _e in range(1, NT):
+    SEMAPHORES += ["rj%d" % _e, "rc%d" % _e, "rl%d" % _e]
+
+VF, SF, CY, PCY, PF, WAKE, SELF, GAP, HOP, GBW = 10.0, 65.0, 0.9, 0.45, 40.0, 80.0, 20.0, 100.0, 1800.0, 250.0
+FIRST = 1e6
+
+
+def program(R, T, topo):
+    ops = []
+    me = T.cores[R]
+
+    def B(name, a, z, step=1):
+        buf, at = PLACE[name]
+        return T[buf][:, at + a:at + z:step] if step > 1 else T[buf][:, at + a:at + z]
+
+    def add(q, dur, reads, writes, calls, sem=None, lat=0.0, tail=0.0, dma=False, bonus=0.0):
+        ops.append({"q": q, "dur": dur, "r": list(reads), "w": list(writes), "calls": calls, "sem": sem, "lat": lat, "tail": tail, "dma": dma, "bonus": bonus})
+        return len(ops) - 1
+
+    def V(cyc, reads, writes, name, *a):
+        call = {"copy": lambda g: g.vector.tensor_copy(*a), "tt": lambda g: g.vector.tensor_tensor(*a),
+                "ts": lambda g: g.vector.tensor_scalar(*a), "set": lambda g: g.vector.memset(*a)}[name]
+        add("v", VF + CY * max(64, cyc), reads, writes, [call])
+
+    def S(cyc, reads, writes, *a, **kw):
+        add("s", SF + CY * max(64, cyc), reads, writes, [lambda g: g.scalar.activation(*a, **kw)])
+
+    def P(reads, writes, mms):
+        cost = PF
+        for m in mms:
+            cost += PCY * max(64, m[5])
+        add("pe", cost, reads, writes, [(lambda g, m=m: g.tensor.matmul(m[0], m[1], m[2], m[3], m[4])) for m in mms])
+
+    def pick(key, out, in_, pat, cmp_, base, cm, el, src):
+        add("g", 170 + 1.9 * el, [src], [key], [lambda g: g.affine_select(out, in_, pat, cmp_, 0.0, base, cm)], sem="kg")
+
+    def D(q, sem, nbytes, reads, writes, out, in_, bonus=0.0):
+        add(q, 100.0, reads, writes, [lambda g: (g.sync if q == "sync" else g.scalar).dma_start(out, in_)],
+            sem=sem, lat=1800.0, tail=nbytes / GBW, dma=True, bonus=bonus)
+
+    def send(dst, sem, nbytes, reads, landing, out, in_, bonus=0.0):
+        core = T.cores[dst % N]
+        rid, pid, _ = topo.addr(core)
+        mk = topo.mask(me, core)
+        k = add("g", 600.0, reads, [], [lambda g: g.remote_dma(out, in_, T.sem[sem], T.sem.ls, pid, rid, mk)], sem="remote", bonus=bonus)
+        j = add("net", 0.0, [], [landing], [], sem=sem, lat=HOP, tail=nbytes / GBW)
+        ops[j]["after"] = k
+        ops[k]["cnt"] = ops[j]["cnt"] = len(topo.engines(me, core))
+
+    for c in range(NCH):
+        D("s", "ly", 16384 // NCH, [], [("y0l", c)], B("y0l", K * c, K * c + K), T.y0[:, n * c:n * c + n], bonus=2 * FIRST)
+    for b in range(JB):
+        D("s", "ljm%d" % b, 128 * JBW * 4, [], [("jmi", b)], T.jmi[:, JBW * b:JBW * b + JBW], T.jm[:, JBW * b:JBW * b + JBW], bonus=FIRST * (1.9 - 0.1 * b))
+    D("sync", "lst", 65536, [], ["sti"], T.sti[:], T.st[:], bonus=2 * FIRST)
+    ltk = []
+    for x in range(N):
+        s = (R - x) % N
+        for c in range(NCH):
+            ltk.append(("lt0", s, c))
+            D("sync", "llt", 16384 // NCH, [], [("lt0", s, c)], B("lt0", 64 * s + K * c, 64 * s + K * c + K), T.lt[:, NK * s + n * c:NK * s + n * c + n], bonus=FIRST)
+    D("sync", "lcf", 128 * W * 2, [], [("C", 0)], T.CW[:, 0:W], T.cf[:], bonus=0.5 * FIRST)
+    yk = [("y0l", c) for c in range(NCH)]
+    V(1024, [], ["ones"], "set", T.ones[:], 1.0)
+    V(1024, [], ["SM0"], "set", T.SM[:], 0.0)
+    for e in range(NT):
+        V(32, [], [("pad", e)], "set", T.CW[:, CWID * e + W:CWID * e + CWID], 0.0)
+    add("g", 1200.0, [], ["io5"], [lambda g: g.iota(T.io5[:], [[1, 576]], 0, 0, allow_small_or_imprecise_dtypes=True)], sem="kg")
+    add("g", 130.0, [], ["ipi"], [lambda g: g.iota(T.ipi[:], [[0, 2]], 0, 1)], sem="kg")
+    V(2, ["ipi"], ["ipj"], "ts", T.ipj[:], T.ipi[:], 15, None, ALU.bitwise_and)
+    V(2, ["ipj"], ["ipf"], "copy", T.ipf[:], T.ipj[:])
+    pick("RM", T.RM[:], T.ones[:], [[-1, 16], [-16, 8], [0, 16]], ALU.is_equal, 0, 1, 2048, "ones")
+    pick("b8a", T.b8a[:], T.ones[:, 0:8], [[-16, 8]], ALU.is_ge, 0, 1, 8, "ones")
+    pick("b8", T.b8[:], T.b8a[:], [[16, 8]], ALU.is_ge, 15, -1, 8, "b8a")
+    pick("ID", T.ID[:], T.ones[:, 0:128], [[-1, 128]], ALU.is_equal, 0, 1, 128, "ones")
+    V(128, ["ID"], ["I4"], "ts", T.I4[:], T.ID[:], 18.0 * HIT / STOP, None, ALU.mult)
+    V(128, ["ID"], ["I8"], "ts", T.I8[:], T.ID[:], -36.0 * HIT / STOP, None, ALU.mult)
+    smk = [("SM", r) for r in range(16)]
+    for r in range(16):
+        V(8, ["b8", "SM0"], [("SM", r)], "ts", T.SM[:, 129 * r:128 * r + 128:16], T.b8[:], HIT, None, ALU.mult)
+    pick("LTa", T.LTa[:], T.ones[:, 0:128], [[-16, 8], [0, 16]], ALU.is_ge, 0, 1, 128, "ones")
+    pick("LTb", T.LTb[:], T.LTa[:], [[16, 8], [0, 16]], ALU.is_ge, 15, -1, 128, "LTa")
+    pick("LTR", T.LTR[:], T.LTb[:], [[1, 128]], ALU.is_gt, 0, -1, 128, "LTb")
+    for bi, be in enumerate((8, 4, 2, 1)):
+        for m, (step, base) in enumerate(((1000, 0), (-1000, 1000), (1000, -be), (-1000, 1000 - be))):
+            j = 4 * bi + m
+            pick(("AM", j), T.AM[:, 128 * j:128 * j + 128], T.ones[:, 0:128], [[-2 * be, 64 // be], [step, 2], [-1, be]], ALU.is_equal, base, 1, 128, "ones")
+    ik = [("I", b) for b in range(8)]
+    for b in range(8):
+        S(576, ["io5"], [("I", b)], T.JW[:, 576 * b:576 * b + 576], T.io5[:], AF.Exp, bias=float(576 * b * SC), scale=float(SC))
+    jk = {0: [("J", 0, b) for b in range(JB)]}
+    lk = {0: ltk}
+    for b in range(JB):
+        a, z = JBW * b, JBW * b + JBW
+        V(JBW, [("jmi", b)], [("jmf", b)], "copy", T.jmf[:, a:z], T.jmi[:, a:z])
+        S(JBW, [("jmf", b)], [("J", 0, b)], T.JW[:, W + a:W + z], T.jmf[:, a:z], AF.Exp, scale=float(SC))
+    for e in range(1, NT):
+        jk[e] = jk[e - 1] + [("J", e)]
+        lk[e] = [("lt", e)]
+        send(R - e, "rl%d" % e, 131072, ltk, ("lt", e), B("lt%d" % e, 0, 512), T.lt0[:], bonus=FIRST)
+    for e in range(1, NT):
+        pace = [("J", e - 1), ("C", e - 1)] if e > 1 else []
+        send(R - e, "rj%d" % e, 128 * W * 2, jk[0] + pace, ("J", e), T.JW[:, W * (1 + e):W * (2 + e)], T.JW[:, W:2 * W], bonus=FIRST if e == 1 else 0.0)
+        send(R - e, "rc%d" % e, 128 * W * 2, [("C", 0)] + pace, ("C", e), T.CW[:, CWID * e:CWID * e + W], T.CW[:, 0:W])
+    wn = [0]
+
+    def wbank():
+        wn[0] += 1
+        return "w%d" % (wn[0] % NCH)
+
+    def smat(r):
+        return T.SM[:, 128 * r:128 * r + 128]
+
+    def rep(src, natural, reads):
+        wb = wbank()
+        P(["RM"] + reads, [wb], [(B(wb, K * r, K * r + K) if natural else B(wb, r, n, 16), T.RM[:, 128 * r:128 * r + 128], src, True, True, K) for r in range(16)])
+        return wb
+
+    def onehot(out, key, src, natural, reads):
+        wb = rep(src, natural, reads)
+        V(n, ["ipf"], [wb, key], "ts", out, B(wb, 0, n), 15.0, T.ipf[:, 0:1], ALU.min, ALU.is_equal)
+
+    def oh_of(off, e, c):
+        a = NK * OHS.index((off, e)) + n * c
+        return T.oh[:, a:a + n], ("oh", off, e, c)
+
+    def slot_letters(off, e):
+        s = (R - off) % N
+        return B("lt%d" % e, 64 * s, 64 * s + 64)
+
+    def onehots(off, e):
+        s = 64 * ((R - off) % N)
+        for c in range(NCH):
+            out, key = oh_of(off, e, c)
+            onehot(out, key, B("lt%d" % e, s + K * c, s + K * c + K), False, lk[e])
+
+    def gates(w, i, x, e, src, reads):
+        es, ej = "es%d%d" % (w, i), "ej%d%d" % (w, i)
+        a = 64 * x
+        big = W * (1 + e) / A
+        V(32, reads, [(es, x)], "ts", B(es, a, a + 64), src, 15.5, STOP, ALU.is_gt, ALU.mult)
+        S(64, [(es, x)], [(ej, x)], B(ej, a, a + 64), B(es, a, a + 64), AF.Copy, bias=float(big), scale=float(-big / STOP))
+
+    for c in range(NCH):
+        onehot(B("ohn", n * c, n * c + n), ("ohn", c), B("y0l", K * c, K * c + K), True, yk)
+    V(128, ["sti"], ["stu"], "copy", T.stu[:], T.sti[:])
+
+    def image(c, lst, lkey, lo, hi, oh, ohk, tk, natural, out, okey):
+        mj, ps = "mj%d" % c, "ps%d" % c
+        V(1.5 * n, [lkey, ohk] + tk, [mj], "tt", B(mj, 0, n), T.JW[:, lo:hi].indirect(lst), oh, ALU.mult)
+        P(smk + [mj], [ps], [(B(ps, 0, K), smat(r), B(mj, K * r, K * r + K) if natural else B(mj, r, n, 16), r == 0, r == 15, K) for r in range(16)])
+        S(K, [], [ps, okey], out, B(ps, 0, K), AF.Ln, scale=float(1.0 / HIT))
+
+    def jlist(c, t, tkey, w, i, x):
+        ej, jl, ta = "ej%d%d" % (w, i), "jl%d" % c, B("ta%d" % c, 0, K)
+        a = 64 * x + K * c
+        V(K, [tkey, (ej, x)], [("jt", c)], "tt", ta, t, B(ej, a, a + K), ALU.add)
+        V(K, [("jt", c)], [jl], "ts", B(jl, 0, K), ta, float(A), None, ALU.mult)
+
+    def gate(c, t, tkey, w, i, x):
+        es = "es%d%d" % (w, i)
+        a = 64 * x + K * c
+        te = B("ta%d" % c, K, 2 * K)
+        V(2 * K, [tkey, (es, x)], [("te", c)], "tt", te, t, B(es, a, a + K), ALU.max)
+        return te, ("te", c)
+
+    def clist(c, te, tek, stop, skeys, touched):
+        t2, cl = B("ta%d" % c, 2 * K, 3 * K), "cl%d" % c
+        V(2 * K, [tek] + skeys, touched + [("t2", c)], "tt", t2, te, stop, ALU.max)
+        V(K, [("t2", c)], [cl], "ts", B(cl, 0, K), t2, float(A), float(A * STOP), ALU.mult, ALU.min)
+
+    def coefs(c, e, out, okey):
+        cl = "cl%d" % c
+        for q in range(NH):
+            S(1.5 * h, [cl, ("C", e), ("pad", e)], [(okey, q)], B(out, h * q, h * q + h),
+              T.CW[:, CWID * e:CWID * e + CWID].indirect(B(cl, K // NH * q, K // NH * (q + 1))), AF.Copy)
+
+    state = [{} for _ in range(NCH)]
+
+    def enter(w, i, off, c, dd):
+        st = state[c]
+        if i == 0:
+            oh = ("ohn", "ohy")[w]
+            tt, cl, vb = "tt%d" % c, "cl%d" % c, "vb%d" % c
+            image(c, B("stu", 64 * w + K * c, 64 * w + K * c + K), "stu", W, 2 * W, B(oh, n * c, n * c + n), (oh, c), jk[0], True, B(tt, 0, K), tt)
+            V(K, [tt], [cl], "ts", B(cl, 0, K), B(tt, 0, K), float(A), None, ALU.mult)
+            coefs(c, 0, vb, vb)
+            st["t"], st["tk"] = B(tt, 0, K), tt
+            st["v"], st["vk"] = vb, [(vb, q) for q in range(NH)]
+            st["dead"] = None
+        else:
+            vi, ti, di = "vi%d%d%d" % (w, i - 1, c), "ti%d%d%d" % (w, i - 1, c), "di%d%d" % (w, i - 1)
+            st["t"], st["tk"] = B(ti, 0, K), ti
+            st["v"], st["vk"] = vi, [vi]
+            st["dead"] = (B(di, K * c, K * c + K), (di, c))
+            S(K, [(di, c)], [(dd, 0, c)], B(dd, K * c, K * c + K), B(di, K * c, K * c + K), AF.Copy)
+
+    def lookup(w, i, off, m, c, slots, k):
+        st = state[c]
+        e, x = slots[k]
+        jl = "jl%d" % c
+        jlist(c, st["t"], st["tk"], w, i, x)
+        if w == 1 and i == 0 and k == 0:
+            oh, ohk = B("ohr", n * c, n * c + n), ("ohr", c)
+        else:
+            oh, ohk = oh_of(off, e, c)
+        hop = k + 1 == len(slots) and i + 1 < len(ST[w])
+        tb = ("to%d%d%d" % (w, i, c)) if hop else ("tt%d" % c)
+        image(c, B(jl, 0, K), jl, 0, W * (2 + e), oh, ohk, ik + jk[e], False, B(tb, 0, K), tb)
+        st["t"], st["tk"] = B(tb, 0, K), tb
+        if hop:
+            ti = "ti%d%d%d" % (w, i, c)
+            send(R + m, "rt%d%d%d" % (w, i, c), 128 * K * 4, [tb], ti, B(ti, 0, K), B(tb, 0, K))
+        st["te"] = gate(c, st["t"], st["tk"], w, i, x)
+
+    def station(w, i, off, m):
+        slots = [(e, e + (1 if w == 1 and i == 0 else 0)) for e in range(m)]
+        if w == 1 and i == 0:
+            slots = [(0, 0)] + slots
+        final = i + 1 == len(ST[w])
+        dst = R - off if final else R + m
+        dd, es = "dd%d%d" % (w, i), "es%d%d" % (w, i)
+        do, di = "do%d%d" % (w, i), "di%d%d" % (w, i)
+        for c in range(NCH):
+            enter(w, i, off, c, dd)
+        for c in range(NCH):
+            lookup(w, i, off, m, c, slots, 0)
+        for k, (e, x) in enumerate(slots):
+            first, last = k == 0, k + 1 == len(slots)
+            nat = last and final
+            for c in range(NCH):
+                st = state[c]
+                cl, cc, sg, ps, vo, vi = "cl%d" % c, "cc%d" % c, "sg%d" % c, "ps%d" % c, "vo%d%d%d" % (w, i, c), "vi%d%d%d" % (w, i, c)
+                pv = ["pv%d%d" % (q, c) for q in range(NH)]
+                te, tek = st["te"]
+                if first and st["dead"] is None:
+                    V(K, [tek], [cl], "ts", B(cl, 0, K), te, float(A), None, ALU.mult)
+                elif first:
+                    clist(c, te, tek, st["dead"][0], [st["dead"][1]], [])
+                v, vk = st["v"], st["vk"]
+                if not nat:
+                    for q in range(NH):
+                        P(["ID"] + vk, [pv[q]], [(B(pv[q], 0, h), T.ID[:], B(v, h * q, h * q + h), True, False, h)])
+                coefs(c, e, cc, cc)
+                for q in range(NH):
+                    if not nat:
+                        P(["ID", (cc, q)], [pv[q]], [(B(pv[q], 0, h), T.ID[:], B(cc, h * q, h * q + h), False, True, h)])
+                    else:
+                        mm = []
+                        for r in range(16 // NH * q, 16 // NH * (q + 1)):
+                            o = B(pv[q], K * r - h * q, K * r - h * q + K)
+                            mm.append((o, T.ID[:], B(v, r, n, 16), True, False, K))
+                            mm.append((o, T.ID[:], B(cc, r, n, 16), False, True, K))
+                        P(["ID"] + [(cc, y) for y in range(NH)] + vk, [pv[q]], mm)
+                vd = vo if last else "vb%d" % c
+                for q in range(NH):
+                    S(h, [], [pv[q], (sg, q)], B(sg, h * q, h * q + h), B(pv[q], 0, h), AF.Sign, bias=0.5)
+                for q in range(NH):
+                    V(h, [], [pv[q], (vd, q)], "ts", B(vd, h * q, h * q + h), B(pv[q], 0, h), 255.0, -255.0, ALU.min, ALU.max)
+                st["v"], st["vk"] = vd, [(vd, q) for q in range(NH)]
+                if last:
+                    send(dst, "rv%d%d%d" % (w, i, c), 128 * n * 2, st["vk"], vi, B(vi, 0, n), B(vo, 0, n))
+                else:
+                    lookup(w, i, off, m, c, slots, k + 1)
+                ea = 64 * x + K * c
+                pk = ["I4", (es, x)]
+                cnt = B(ps, K, 2 * K)
+                mm = [(cnt, T.I4[:], B(es, ea, ea + K), True, False, K)]
+                if st["dead"] is not None:
+                    mm.append((cnt, T.I8[:], st["dead"][0], False, False, K))
+                    pk += ["I8", st["dead"][1]]
+                for r in range(16):
+                    mm.append((cnt, smat(r), B(sg, K * r, K * r + K) if nat else B(sg, r, n, 16), False, r == 15, K))
+                P(smk + pk + [(sg, q) for q in range(NH)], [ps], mm)
+                a, z = 64 * (x + 1) + K * c, K * c
+                if not last:
+                    te, tek = st["te"]
+                    clist(c, te, tek, cnt, [], [ps])
+                    V(K, [], [ps, (dd, x + 1, c)], "ts", B(dd, a, a + K), cnt, -HIT, STOP, ALU.is_gt, ALU.mult)
+                    st["dead"] = (B(dd, a, a + K), (dd, x + 1, c))
+                else:
+                    V(K, [], [ps, (do, c)], "ts", B(do, z, z + K), cnt, -HIT, STOP, ALU.is_gt, ALU.mult)
+                    send(dst, "rd%d%d%d" % (w, i, c), 128 * K * 2, [(do, c)], (di, c), B(di, z, z + K), B(do, z, z + K))
+                    S(K, [(do, c)], [(dd, x + 1, c)], B(dd, a, a + K), B(do, z, z + K), AF.Copy)
+        settle(w, i, off, dd, slots)
+
+    def store_yl(s, buf, a, key):
+        for c in range(NCH):
+            D("sync", "stores", 16384 // NCH, [key], [("out",)], T.yl[:, NK * s + n * c:NK * s + n * c + n], B(buf, a + K * c, a + K * c + K))
+
+    src1 = {}
+
+    def settle(w, i, off, dd, slots):
+        hi, ls = "hi%d%d" % (w, i), "ls%d%d" % (w, i)
+        for e, x in slots:
+            if w == 1 and i == 0 and x == 0:
+                continue
+            b = 64 * x
+            dk = [(dd, x + 1, c) for c in range(NCH)]
+            if i == 0 and x == 0:
+                hit, hk = B(dd, 64, 128), dk
+            else:
+                V(128, dk + [(dd, x, c) for c in range(NCH)], [(hi, x)], "tt", B(hi, b, b + 64), B(dd, b + 64, b + 128), B(dd, b, b + 64), ALU.subtract)
+                hit, hk = B(hi, b, b + 64), [(hi, x)]
+            src, sk = (slot_letters(off, e), lk[e]) if w == 0 else src1[(i, e)]
+            o = B(ls, 64 * e, 64 * e + 64)
+            V(128, sk + hk, [(ls, e)], "tt", o, src, hit, ALU.max)
+            if w == 1:
+                V(32, [(ls, e)], [("yo", i, e)], "ts", o, o, 16.0, None, ALU.min)
+                if e == 0:
+                    store_yl((R - off) % N, ls, 0, ("yo", i, 0))
+                else:
+                    yr = "yr%d%d" % (i, e)
+                    send(R + e, "ry%d%d" % (i, e), 16384, [("yo", i, e)], yr, B(yr, 0, 64), o)
+                    store_yl((R - e - off) % N, yr, 0, yr)
+        if w == 0:
+            for a, b, lo, hh in MOVES:
+                if a == i:
+                    mv = "mv%d%d" % (a, b)
+                    send(R - off + ST[1][b][0], "rmv%d%d" % (a, b), 16384 * (hh - lo), [(ls, d - off) for d in range(lo, hh)], mv,
+                         B(mv, 0, 64 * (hh - lo)), B(ls, 64 * (lo - off), 64 * (hh - off)))
+
+    done = []
+    for i, (off, m) in enumerate(ST[0]):
+        for e in range(m):
+            gates(0, i, e, e, slot_letters(off, e), lk[e])
+            onehots(off, e)
+            done.append((off, e))
+        if i + 1 == len(ST[0]):
+            for q in OHS:
+                if q not in done:
+                    onehots(q[0], q[1])
+            for c in range(NCH):
+                onehot(B("ohr", n * c, n * c + n), ("ohr", c), B("y0l", K * c, K * c + K), False, yk)
+        station(0, i, off, m)
+    hv, hd = "vi0%d" % (len(ST[0]) - 1), "di0%d" % (len(ST[0]) - 1)
+    for c in range(NCH):
+        a = K * c
+        V(K, [(hd, c)], [("es10", 0)], "copy", B("es10", a, a + K), B(hd, a, a + K))
+        S(K, [(hd, c)], [("ej10", 0)], B("ej10", a, a + K), B(hd, a, a + K), AF.Copy, bias=float(W / A), scale=float(-W / A / STOP))
+    for b, (off, m) in enumerate(ST[1]):
+        for e in range(m):
+            d = off + e
+            for a, (o0, m0) in enumerate(ST[0]):
+                if o0 <= d < o0 + m0:
+                    if o0 == off:
+                        ap, key = B("ls0%d" % a, 64 * (d - o0), 64 * (d - o0) + 64), [("ls0%d" % a, d - o0)]
+                    else:
+                        lo = max(o0, off)
+                        ap, key = B("mv%d%d" % (a, b), 64 * (d - lo), 64 * (d - lo) + 64), ["mv%d%d" % (a, b)]
+            src1[(b, e)] = (ap, key)
+            gates(1, b, e + (1 if b == 0 else 0), e, ap, key)
+    for c in range(NCH):
+        vi = hv + str(c)
+        ax, am = "ax%d" % c, "am%d" % c
+        src, sk, wd, pos = vi, vi, n, 0
+        for bi in range(4):
+            hf = wd // 2
+            wb = wbank()
+            mm = []
+            for j in range(2):
+                for k in range(2):
+                    q = 4 * bi + 2 * j + k
+                    mm.append((B(wb, hf * j, hf * j + hf), T.AM[:, 128 * q:128 * q + 128], B(src, pos + hf * k, pos + hf * k + hf), k == 0, k == 1, hf))
+            P([("AM", 4 * bi + y) for y in range(4)] + [sk], [wb], mm)
+            S(hf, [], [wb, ax], B(ax, 0, hf), B(wb, 0, hf), AF.Copy)
+            npos = 0 if bi == 0 else pos + wd
+            V(hf, [ax], [wb, (am, bi)], "tt", B(am, npos, npos + hf), B(ax, 0, hf), B(wb, hf, 2 * hf), ALU.max)
+            src, sk, wd, pos = am, (am, bi), hf, npos
+        wb = rep(B(am, pos, pos + K), True, [(am, 3)])
+        V(n, [vi], [wb, (am, "eq")], "tt", B(am, n, 2 * n), B(vi, 0, n), B(wb, 0, n), ALU.is_equal)
+        w2 = wbank()
+        P(["LTR", (am, "eq")], [w2], [(B(w2, 0, n), T.LTR[:], B(am, n, 2 * n), True, True, n)])
+        V(n, [(am, "eq")], [w2, ("ohy", c)], "tt", B("ohy", n * c, n * c + n), B(am, n, 2 * n), B(w2, 0, n), ALU.is_gt)
+    for i, (off, m) in enumerate(ST[1]):
+        station(1, i, off, m)
+    for c in range(NCH):
+        ax, d1, v1 = "ax%d" % c, "di1%d" % (len(ST[1]) - 1), "vi1%d%d" % (len(ST[1]) - 1, c)
+        a = K * c
+        S(n, [("ohy", c), "ipf"], [ax], B(ax, 0, n), B("ohy", n * c, n * c + n), AF.Copy, scale=T.ipf[:, 0:1])
+        wb = wbank()
+        P(smk + [ax], [wb], [(B(wb, 0, K), smat(r), B(ax, K * r, K * r + K), r == 0, r == 15, K) for r in range(16)])
+        y1, ym = B("y1l", a, a + K), B("yim", a, a + K)
+        V(K, [], [wb, ("y1l", c)], "ts", y1, B(wb, 0, K), float(1.0 / HIT), None, ALU.mult)
+        V(K, [("y0l", c), (hd, c)], [("yim", c)], "tt", ym, B("y0l", a, a + K), B(hd, a, a + K), ALU.max)
+        V(K, [("yim", c), ("dd10", 1, c)], [("yiu", c)], "tt", ym, ym, B("dd10", 64 + a, 64 + a + K), ALU.max)
+        V(K, [("yiu", c)], [("yi0", c)], "ts", B("yit", a, a + K), ym, 16.0, None, ALU.min)
+        V(K, [("y1l", c), (d1, c)], [("y1m", c)], "tt", y1, y1, B(d1, a, a + K), ALU.max)
+        V(K, [("y1m", c)], [("yi1", c)], "ts", B("yit", 64 + a, 64 + a + K), y1, 16.0, None, ALU.min)
+        for t in range(2):
+            D("sync", "stores", 16384 // NCH, [("yi%d" % t, c)], [("out",)], T.yi[:, NK * t + n * c:NK * t + n * c + n], B("yit", 64 * t + a, 64 * t + a + K))
+        D("sync", "stores", 128 * n * 2, [v1], [("out",)], T.yv[:, n * c:n * c + n], B(v1, 0, n))
+    return ops
+
+
+def depend(ops):
+    writer, readers = {}, {}
+    for k, o in enumerate(ops):
+        d = {}
+        for key in o["r"]:
+            for x in writer.get(key, []):
+                d[x] = True
+        for key in o["w"]:
+            if key == ("out",):
+                continue
+            for x in writer.get(key, []) + readers.get(key, []):
+                d.setdefault(x, False)
+        if "after" in o:
+            d[o["after"]] = True
+        o["d"] = d
+        for key in o["w"]:
+            if key in (("es10", 0), ("ej10", 0)):
+                writer.setdefault(key, []).append(k)
+            else:
+                writer[key] = [k]
+            readers[key] = []
+        for key in o["r"]:
+            readers.setdefault(key, []).append(k)
+
+
+def order(ops):
+    cnt = len(ops)
+    nxt = [[] for _ in range(cnt)]
+    for k, o in enumerate(ops):
+        for x in o["d"]:
+            nxt[x].append(k)
+    prio = [0.0] * cnt
+    for k in range(cnt - 1, -1, -1):
+        o = ops[k]
+        best = 0.0
+        for y in nxt[k]:
+            best = max(best, prio[y] + WAKE)
+        prio[k] = best + o["dur"] + o["lat"] + o["tail"]
+    left = [len(o["d"]) for o in ops]
+    ready = [0.0] * cnt
+    cand = {}
+    for k in range(cnt):
+        if left[k] == 0:
+            cand.setdefault(ops[k]["q"], []).append(k)
+    free, lane, out = {}, 0.0, []
+
+    def rank(x):
+        return prio[x] + ops[x]["bonus"]
+    while cand:
+        t, q = None, None
+        for y in cand:
+            f = max(free.get(y, 0.0) if y != "net" else 0.0, min(ready[k] for k in cand[y]))
+            if t is None or f < t:
+                t, q = f, y
+        k = max((x for x in cand[q] if ready[x] <= t + (GAP if q != "net" else 0.0)), key=rank)
+        if ready[k] > t:
+            fit = [x for x in cand[q] if ready[x] <= t and t + ops[x]["dur"] <= ready[k] + 20.0]
+            if fit:
+                k = max(fit, key=rank)
+            else:
+                t = ready[k]
+        cand[q].remove(k)
+        if not cand[q]:
+            del cand[q]
+        o = ops[k]
+        end = t + o["dur"]
+        free[q] = end
+        if o["tail"]:
+            lane = max(end, lane) + o["tail"]
+            end = lane + o["lat"]
+        out.append(k)
+        for y in nxt[k]:
+            left[y] -= 1
+            ready[y] = max(ready[y], end + (WAKE if ops[y]["q"] != q else SELF))
+            if left[y] == 0:
+                cand.setdefault(ops[y]["q"], []).append(y)
+    return out
+
+
+QSEM = {"pe": "kpe", "v": "kv", "s": "ks"}
+
+
+def rank_program(g, core, T, topo):
+    rank = T.rank_of(core)
+    if rank is None:
+        return
+    ops = program(rank, T, topo)
+    depend(ops)
+    seq = order(ops)
+    total = {}
+    for o in ops:
+        if o["dma"]:
+            total[o["sem"]] = total.get(o["sem"], 0) + 16
+    eng = {"pe": g.tensor, "v": g.vector, "s": g.scalar, "g": g, "sync": g.sync}
+    count, sent, arrived, know = {}, 0, {}, {}
+    for k in seq:
+        o = ops[k]
+        q = o["q"]
+        if q == "net":
+            o["done"] = [(o["sem"], o["cnt"])]
+            o["know"] = {o["sem"]: o["cnt"]}
+            arrived[o["sem"]] = o["cnt"]
+            continue
+        mine = know.setdefault(q, {})
+        need, merge = {}, []
+        for x, hard in o["d"].items():
+            p = ops[x]
+            if p["sem"] == "remote" or (not hard and p["q"] == q == "pe"):
+                continue
+            for s, c in p["done"]:
+                if mine.get(s, 0) < c:
+                    need[s] = max(need.get(s, 0), c)
+            merge.append(x)
+        for s in sorted(need):
+            implied = False
+            for x in merge:
+                if ops[x]["know"].get(s, 0) >= need[s] and ops[x]["done"][0][0] != s:
+                    implied = True
+            if not implied:
+                eng[q].wait_ge(T.sem[s], int(need[s]))
+        for x in merge:
+            for s, c in ops[x]["know"].items():
+                mine[s] = max(mine.get(s, 0), c)
+        sem = o["sem"] or QSEM.get(q)
+        for call in o["calls"]:
+            ins = call(g)
+            if sem == "remote":
+                sent += o["cnt"]
+            elif o["dma"]:
+                ins.then_inc(T.sem[sem], 16)
+            else:
+                count[sem] = count.get(sem, 0) + 1
+                ins.then_inc(T.sem[sem], 1)
+        o["know"] = dict(mine)
+        if sem == "remote":
+            o["done"] = []
+            continue
+        c = total[sem] if o["dma"] else count[sem]
+        o["done"] = [(sem, c)]
+        o["know"][sem] = max(o["know"].get(sem, 0), c)
+    for s in ("kpe", "kv", "ks", "kg"):
+        g.wait_ge(T.sem[s], int(count[s]))
+    for s in sorted(total):
+        g.wait_ge(T.sem[s], int(total[s]))
+    for s in sorted(arrived):
+        g.wait_ge(T.sem[s], int(arrived[s]))
+    g.wait_ge(T.sem.ls, int(sent))

@@ -126,12 +126,23 @@ for _i, (_o, _m) in enumerate(ST[1]):
 for _e in range(1, NT):
     SEMAPHORES += ["rj%d" % _e, "rc%d" % _e, "rl%d" % _e]
 
-VF, SF, CY, PCY, PF, WAKE, SELF, GAP, HOP, GBW = 10.0, 65.0, 0.9, 0.45, 40.0, 80.0, 20.0, 100.0, 1800.0, 250.0
+VF, SF, CY, PCY, PF, WAKE, SELF, GAP, HOP, GBW = 5.0, 65.0, 0.95, 0.5, 20.0, 80.0, 40.0, 200.0, 1800.0, 250.0
 FIRST = 1e6
+URGE = {
+    0: {"cc": 600, "cl": 1000, "dd": 1200, "di": -9900, "do": 500, "jl": 3800, "jt": 200, "mj": 1400, "ps": 1400, "psc": -3400, "pv": 900,
+        "sg": 1000, "t": 300, "te": 600, "ti": 100, "to": 1000, "tt": 8900, "vb": -1800, "vi": -14900, "vo": 1700},
+    1: {"dd": 800, "ti": 12400, "mj": 1000, "vi": -5400, "psc": 17000, "te": -200, "t": 700, "jl": -3500, "cl": 3600, "pv": 300, "di": -9700,
+        "ps": 200, "to": 300, "tt": 6600, "sg": 200, "jt": -2400, "vb": 300, "do": 500, "vo": 200},
+    None: {"LTa": -3800, "out": -1500, "ax": -6000, "ipf": 2800, "b8a": -3500, "pad": -1900, "w": -5300, "ohr": 600, "y1l": 22900, "am": -3600,
+           "stu": -1000, "ipi": 15600, "jmf": 5000, "ej": -800, "sti": -6200, "hi": -5000, "ones": -3000, "yo": -26700, "yi": -10000, "yim": -3300,
+           "ID": -21000, "io": 10800, "y0l": 7600, "b": -16500, "ipj": -24300, "LTR": 2100, "jmi": 5800, "RM": 15700, "yiu": -11200, "ls": -8100,
+           "SM": 900, "ohn": -4900, "LTb": -11800, "y1m": 4200, "lt": 9700, "AM": -6200, "ohy": -100, "J": -6200, "I": -1800, "C": -7300, "oh": 300, "es": 600},
+}
 
 
 def program(R, T, topo):
     ops = []
+    cur = [None]
     me = T.cores[R]
 
     def B(name, a, z, step=1):
@@ -139,7 +150,7 @@ def program(R, T, topo):
         return T[buf][:, at + a:at + z:step] if step > 1 else T[buf][:, at + a:at + z]
 
     def add(q, dur, reads, writes, calls, sem=None, lat=0.0, tail=0.0, dma=False, bonus=0.0):
-        ops.append({"q": q, "dur": dur, "r": list(reads), "w": list(writes), "calls": calls, "sem": sem, "lat": lat, "tail": tail, "dma": dma, "bonus": bonus})
+        ops.append({"q": q, "dur": dur, "r": list(reads), "w": list(writes), "calls": calls, "sem": sem, "lat": lat, "tail": tail, "dma": dma, "bonus": bonus, "ch": cur[0]})
         return len(ops) - 1
 
     def V(cyc, reads, writes, name, *a):
@@ -159,9 +170,8 @@ def program(R, T, topo):
     def pick(key, out, in_, pat, cmp_, base, cm, el, src):
         add("g", 170 + 1.9 * el, [src], [key], [lambda g: g.affine_select(out, in_, pat, cmp_, 0.0, base, cm)], sem="kg")
 
-    def D(q, sem, nbytes, reads, writes, out, in_, bonus=0.0):
-        add(q, 100.0, reads, writes, [lambda g: (g.sync if q == "sync" else g.scalar).dma_start(out, in_)],
-            sem=sem, lat=1800.0, tail=nbytes / GBW, dma=True, bonus=bonus)
+    def D(sem, nbytes, reads, writes, out, in_, bonus=0.0):
+        add("sync", 100.0, reads, writes, [lambda g: g.sync.dma_start(out, in_)], sem=sem, lat=1800.0, tail=nbytes / GBW, dma=True, bonus=bonus)
 
     def send(dst, sem, nbytes, reads, landing, out, in_, bonus=0.0):
         core = T.cores[dst % N]
@@ -173,17 +183,16 @@ def program(R, T, topo):
         ops[k]["cnt"] = ops[j]["cnt"] = len(topo.engines(me, core))
 
     for c in range(NCH):
-        D("s", "ly", 16384 // NCH, [], [("y0l", c)], B("y0l", K * c, K * c + K), T.y0[:, n * c:n * c + n], bonus=2 * FIRST)
+        D("ly", 16384 // NCH, [], [("y0l", c)], B("y0l", K * c, K * c + K), T.y0[:, n * c:n * c + n], bonus=9 * FIRST)
+    ltk = [("lt0", (R - x) % N, c) for x in range(N) for c in range(NCH)]
+    per = -(-len(ltk) // (JB - 1))
     for b in range(JB):
-        D("s", "ljm%d" % b, 128 * JBW * 4, [], [("jmi", b)], T.jmi[:, JBW * b:JBW * b + JBW], T.jm[:, JBW * b:JBW * b + JBW], bonus=FIRST * (1.9 - 0.1 * b))
-    D("sync", "lst", 65536, [], ["sti"], T.sti[:], T.st[:], bonus=2 * FIRST)
-    ltk = []
-    for x in range(N):
-        s = (R - x) % N
-        for c in range(NCH):
-            ltk.append(("lt0", s, c))
-            D("sync", "llt", 16384 // NCH, [], [("lt0", s, c)], B("lt0", 64 * s + K * c, 64 * s + K * c + K), T.lt[:, NK * s + n * c:NK * s + n * c + n], bonus=FIRST)
-    D("sync", "lcf", 128 * W * 2, [], [("C", 0)], T.CW[:, 0:W], T.cf[:], bonus=0.5 * FIRST)
+        D("ljm%d" % b, 128 * JBW * 4, [], [("jmi", b)], T.jmi[:, JBW * b:JBW * b + JBW], T.jm[:, JBW * b:JBW * b + JBW], bonus=FIRST * (8.5 - b))
+        for _, s, c in ltk[per * b:per * b + per]:
+            D("llt", 16384 // NCH, [], [("lt0", s, c)], B("lt0", 64 * s + K * c, 64 * s + K * c + K), T.lt[:, NK * s + n * c:NK * s + n * c + n], bonus=FIRST * (8.0 - b))
+        if b == 0:
+            D("lst", 65536, [], ["sti"], T.sti[:], T.st[:], bonus=8 * FIRST)
+    D("lcf", 128 * W * 2, [], [("C", 0)], T.CW[:, 0:W], T.cf[:], bonus=2 * FIRST)
     yk = [("y0l", c) for c in range(NCH)]
     V(1024, [], ["ones"], "set", T.ones[:], 1.0)
     V(1024, [], ["SM0"], "set", T.SM[:], 0.0)
@@ -303,6 +312,7 @@ def program(R, T, topo):
 
     def enter(w, i, off, c, dd):
         st = state[c]
+        cur[0] = c
         if i == 0:
             oh = ("ohn", "ohy")[w]
             tt, cl, vb = "tt%d" % c, "cl%d" % c, "vb%d" % c
@@ -321,6 +331,7 @@ def program(R, T, topo):
 
     def lookup(w, i, off, m, c, slots, k):
         st = state[c]
+        cur[0] = c
         e, x = slots[k]
         jl = "jl%d" % c
         jlist(c, st["t"], st["tk"], w, i, x)
@@ -354,6 +365,7 @@ def program(R, T, topo):
             nat = last and final
             for c in range(NCH):
                 st = state[c]
+                cur[0] = c
                 cl, cc, sg, ps, vo, vi = "cl%d" % c, "cc%d" % c, "sg%d" % c, "ps%d" % c, "vo%d%d%d" % (w, i, c), "vi%d%d%d" % (w, i, c)
                 pv = ["pv%d%d" % (q, c) for q in range(NH)]
                 te, tek = st["te"]
@@ -406,11 +418,12 @@ def program(R, T, topo):
                     V(K, [], [ps, (do, c)], "ts", B(do, z, z + K), cnt, -HIT, STOP, ALU.is_gt, ALU.mult)
                     send(dst, "rd%d%d%d" % (w, i, c), 128 * K * 2, [(do, c)], (di, c), B(di, z, z + K), B(do, z, z + K))
                     S(K, [(do, c)], [(dd, x + 1, c)], B(dd, a, a + K), B(do, z, z + K), AF.Copy)
+        cur[0] = None
         settle(w, i, off, dd, slots)
 
     def store_yl(s, buf, a, key):
         for c in range(NCH):
-            D("sync", "stores", 16384 // NCH, [key], [("out",)], T.yl[:, NK * s + n * c:NK * s + n * c + n], B(buf, a + K * c, a + K * c + K))
+            D("stores", 16384 // NCH, [key], [("out",)], T.yl[:, NK * s + n * c:NK * s + n * c + n], B(buf, a + K * c, a + K * c + K))
 
     src1 = {}
 
@@ -444,18 +457,17 @@ def program(R, T, topo):
                     send(R - off + ST[1][b][0], "rmv%d%d" % (a, b), 16384 * (hh - lo), [(ls, d - off) for d in range(lo, hh)], mv,
                          B(mv, 0, 64 * (hh - lo)), B(ls, 64 * (lo - off), 64 * (hh - off)))
 
-    done = []
     for i, (off, m) in enumerate(ST[0]):
         for e in range(m):
             gates(0, i, e, e, slot_letters(off, e), lk[e])
-            onehots(off, e)
-            done.append((off, e))
-        if i + 1 == len(ST[0]):
-            for q in OHS:
-                if q not in done:
-                    onehots(q[0], q[1])
+    for e in range(NT):
+        for q in OHS:
+            if q[1] == e:
+                onehots(q[0], e)
+        if e == 0:
             for c in range(NCH):
                 onehot(B("ohr", n * c, n * c + n), ("ohr", c), B("y0l", K * c, K * c + K), False, yk)
+    for i, (off, m) in enumerate(ST[0]):
         station(0, i, off, m)
     hv, hd = "vi0%d" % (len(ST[0]) - 1), "di0%d" % (len(ST[0]) - 1)
     for c in range(NCH):
@@ -512,8 +524,8 @@ def program(R, T, topo):
         V(K, [("y1l", c), (d1, c)], [("y1m", c)], "tt", y1, y1, B(d1, a, a + K), ALU.max)
         V(K, [("y1m", c)], [("yi1", c)], "ts", B("yit", 64 + a, 64 + a + K), y1, 16.0, None, ALU.min)
         for t in range(2):
-            D("sync", "stores", 16384 // NCH, [("yi%d" % t, c)], [("out",)], T.yi[:, NK * t + n * c:NK * t + n * c + n], B("yit", 64 * t + a, 64 * t + a + K))
-        D("sync", "stores", 128 * n * 2, [v1], [("out",)], T.yv[:, n * c:n * c + n], B(v1, 0, n))
+            D("stores", 16384 // NCH, [("yi%d" % t, c)], [("out",)], T.yi[:, NK * t + n * c:NK * t + n * c + n], B("yit", 64 * t + a, 64 * t + a + K))
+        D("stores", 128 * n * 2, [v1], [("out",)], T.yv[:, n * c:n * c + n], B(v1, 0, n))
     return ops
 
 
@@ -542,6 +554,12 @@ def depend(ops):
             readers.setdefault(key, []).append(k)
 
 
+def kind(o):
+    name = o["w"][-1] if o["w"] else (o["r"][0] if o["r"] else "")
+    name = (name if isinstance(name, str) else name[0]).rstrip("0123456789")
+    return name + ("c" if o["q"] == "pe" and any(str(x[0]).startswith("sg") for x in o["r"]) else "")
+
+
 def order(ops):
     cnt = len(ops)
     nxt = [[] for _ in range(cnt)]
@@ -555,6 +573,7 @@ def order(ops):
         for y in nxt[k]:
             best = max(best, prio[y] + WAKE)
         prio[k] = best + o["dur"] + o["lat"] + o["tail"]
+    urge = [prio[k] + o["bonus"] + URGE[o["ch"]].get(kind(o), 0) for k, o in enumerate(ops)]
     left = [len(o["d"]) for o in ops]
     ready = [0.0] * cnt
     cand = {}
@@ -564,7 +583,7 @@ def order(ops):
     free, lane, out = {}, 0.0, []
 
     def rank(x):
-        return prio[x] + ops[x]["bonus"]
+        return urge[x]
     while cand:
         t, q = None, None
         for y in cand:

import math
from concourse.mybir import AluOpType, ActivationFunctionType

ALU, AF = AluOpType, ActivationFunctionType
N, W, NK = 8, 4608, 1024
NCH = 2
n = NK // NCH
K = n // 16
NH = 2
h = n // NH
PLAN = [[2, 2, 2, 2], [2, 2, 2, 2]]
NT = max(max(p) for p in PLAN)
CWID = W + 32
PER = 72.0
SC = math.log(2.0) / PER
A = PER / math.log(2.0)
HIT = -22.25
STOP = 44.5
JB = 6
JBW = W // JB
B16, F32, I32, U16 = "bfloat16", "float32", "int32", "uint16"

ST = []
for _w in range(2):
    _o, _l = 0, []
    for _m in PLAN[_w]:
        _l.append((_o, _m))
        _o += _m
    ST.append(_l)


def nslots(w, i):
    return ST[w][i][1] + (1 if w == 1 and i == 0 else 0)


SCRATCH, SEMAPHORES = {}, ["kpe", "kv", "ks", "kg", "ls", "lcf", "lst", "llt", "ly", "stores"]
PLACE = {}


def sb(name, cols, dtype=B16):
    SCRATCH[name] = ("sbuf", [128, cols], dtype)
    PLACE[name] = (name, 0)


def tile(kind, key, cols, dtype=B16):
    buf = "z" + kind
    at = SCRATCH[buf][1][1] if buf in SCRATCH else 0
    SCRATCH[buf] = ("sbuf", [128, at + cols], dtype)
    PLACE[kind + key] = (buf, at)


sb("JW", (1 + NT) * W)
sb("CW", NT * CWID)
sb("jmi", W, I32)
sb("jmf", W, F32)
sb("io5", 576, F32)
for _k in ("ones", "RM", "SM", "AM"):
    sb(_k, 2048)
for _k in ("ID", "I4", "I8", "LTa", "LTb", "LTR"):
    sb(_k, 128)
sb("b8a", 8)
sb("b8", 8)
sb("ipi", 2, I32)
sb("ipj", 2, I32)
sb("ipf", 2, F32)
sb("sti", 128, I32)
sb("stu", 128, U16)
for _k in ("y0l", "y1l", "yim"):
    sb(_k, 64)
sb("yit", 128)
for _k in ("ohn", "ohy", "ohr"):
    sb(_k, NK)
SEMAPHORES += ["ljm%d" % _b for _b in range(JB)]
for _e in range(NT):
    sb("lt%d" % _e, 512)
for _c in range(NCH):
    for _k in ("mj", "sg", "cc", "vb", "ax"):
        sb("%s%d" % (_k, _c), n)
    sb("am%d" % _c, 2 * n)
    sb("tt%d" % _c, K, F32)
    sb("ta%d" % _c, 3 * K, F32)
    sb("jl%d" % _c, K, U16)
    sb("cl%d" % _c, K, U16)
    for _k in ["ps", "w"] + ["pv%d" % _x for _x in range(NH)]:
        SCRATCH["%s%d" % (_k, _c)] = ("psum", [128, 512], F32)
        PLACE["%s%d" % (_k, _c)] = ("%s%d" % (_k, _c), 0)
OHS = []
for _w in range(2):
    for _o, _m in ST[_w]:
        for _e in range(_m):
            if (_o, _e) not in OHS:
                OHS.append((_o, _e))
sb("oh", NK * len(OHS))
MOVES = []
for _i, (_o, _m) in enumerate(ST[0]):
    for _k, (_p, _q) in enumerate(ST[1]):
        _lo, _hi = max(_o, _p), min(_o + _m, _p + _q)
        if _o != _p and _lo < _hi:
            MOVES.append((_i, _k, _lo, _hi))
            tile("mv", "%d%d" % (_i, _k), 64 * (_hi - _lo))
            SEMAPHORES.append("rmv%d%d" % (_i, _k))
for _w in range(2):
    for _i, (_o, _m) in enumerate(ST[_w]):
        _s = nslots(_w, _i)
        _x = "%d%d" % (_w, _i)
        tile("dd", _x, 64 * (_s + 1))
        tile("es", _x, 64 * _s)
        tile("ej", _x, 64 * _s, F32)
        tile("hi", _x, 64 * _s)
        tile("ls", _x, 64 * _m)
        tile("do", _x, 64)
        tile("di", _x, 64)
        for _c in range(NCH):
            _y = "%s%d" % (_x, _c)
            tile("vo", _y, n)
            tile("vi", _y, n)
            SEMAPHORES += ["rv" + _y, "rd" + _y]
            if _i + 1 < len(ST[_w]):
                tile("to", _y, K, F32)
                tile("ti", _y, K, F32)
                SEMAPHORES.append("rt" + _y)
for _i, (_o, _m) in enumerate(ST[1]):
    for _e in range(1, _m):
        tile("yr", "%d%d" % (_i, _e), 64)
        SEMAPHORES.append("ry%d%d" % (_i, _e))
for _e in range(1, NT):
    SEMAPHORES += ["rj%d" % _e, "rc%d" % _e, "rl%d" % _e]

VF, SF, CY, PCY, PF, WAKE, SELF, GAP, HOP, GBW = 5.0, 65.0, 0.95, 0.5, 20.0, 80.0, 40.0, 200.0, 1800.0, 250.0
FIRST = 1e6
URGE = {
    0: {"cc": 600, "cl": 1000, "dd": 1200, "di": -9900, "do": 500, "jl": 3800, "jt": 200, "mj": 1400, "ps": 1400, "psc": -3400, "pv": 900,
        "sg": 1000, "t": 300, "te": 600, "ti": 100, "to": 1000, "tt": 8900, "vb": -1800, "vi": -14900, "vo": 1700},
    1: {"dd": 800, "ti": 12400, "mj": 1000, "vi": -5400, "psc": 17000, "te": -200, "t": 700, "jl": -3500, "cl": 3600, "pv": 300, "di": -9700,
        "ps": 200, "to": 300, "tt": 6600, "sg": 200, "jt": -2400, "vb": 300, "do": 500, "vo": 200},
    None: {"LTa": -3800, "out": -1500, "ax": -6000, "ipf": 2800, "b8a": -3500, "pad": -1900, "w": -5300, "ohr": 600, "y1l": 22900, "am": -3600,
           "stu": -1000, "ipi": 15600, "jmf": 5000, "ej": -800, "sti": -6200, "hi": -5000, "ones": -3000, "yo": -26700, "yi": -10000, "yim": -3300,
           "ID": -21000, "io": 10800, "y0l": 7600, "b": -16500, "ipj": -24300, "LTR": 2100, "jmi": 5800, "RM": 15700, "yiu": -11200, "ls": -8100,
           "SM": 900, "ohn": -4900, "LTb": -11800, "y1m": 4200, "lt": 9700, "AM": -6200, "ohy": -100, "J": -6200, "I": -1800, "C": -7300, "oh": 300, "es": 600},
}


def program(R, T, topo):
    ops = []
    cur = [None]
    me = T.cores[R]

    def B(name, a, z, step=1):
        buf, at = PLACE[name]
        return T[buf][:, at + a:at + z:step] if step > 1 else T[buf][:, at + a:at + z]

    def add(q, dur, reads, writes, calls, sem=None, lat=0.0, tail=0.0, dma=False, bonus=0.0):
        ops.append({"q": q, "dur": dur, "r": list(reads), "w": list(writes), "calls": calls, "sem": sem, "lat": lat, "tail": tail, "dma": dma, "bonus": bonus, "ch": cur[0]})
        return len(ops) - 1

    def V(cyc, reads, writes, name, *a):
        call = {"copy": lambda g: g.vector.tensor_copy(*a), "tt": lambda g: g.vector.tensor_tensor(*a),
                "ts": lambda g: g.vector.tensor_scalar(*a), "set": lambda g: g.vector.memset(*a)}[name]
        add("v", VF + CY * max(64, cyc), reads, writes, [call])

    def S(cyc, reads, writes, *a, **kw):
        add("s", SF + CY * max(64, cyc), reads, writes, [lambda g: g.scalar.activation(*a, **kw)])

    def P(reads, writes, mms):
        cost = PF
        for m in mms:
            cost += PCY * max(64, m[5])
        add("pe", cost, reads, writes, [(lambda g, m=m: g.tensor.matmul(m[0], m[1], m[2], m[3], m[4])) for m in mms])

    def pick(key, out, in_, pat, cmp_, base, cm, el, src):
        add("g", 170 + 1.9 * el, [src], [key], [lambda g: g.affine_select(out, in_, pat, cmp_, 0.0, base, cm)], sem="kg")

    def D(sem, nbytes, reads, writes, out, in_, bonus=0.0):
        add("sync", 100.0, reads, writes, [lambda g: g.sync.dma_start(out, in_)], sem=sem, lat=1800.0, tail=nbytes / GBW, dma=True, bonus=bonus)

    def send(dst, sem, nbytes, reads, landing, out, in_, bonus=0.0):
        core = T.cores[dst % N]
        rid, pid, _ = topo.addr(core)
        mk = topo.mask(me, core)
        k = add("g", 600.0, reads, [], [lambda g: g.remote_dma(out, in_, T.sem[sem], T.sem.ls, pid, rid, mk)], sem="remote", bonus=bonus)
        j = add("net", 0.0, [], [landing], [], sem=sem, lat=HOP, tail=nbytes / GBW)
        ops[j]["after"] = k
        ops[k]["cnt"] = ops[j]["cnt"] = len(topo.engines(me, core))

    for c in range(NCH):
        D("ly", 16384 // NCH, [], [("y0l", c)], B("y0l", K * c, K * c + K), T.y0[:, n * c:n * c + n], bonus=9 * FIRST)
    ltk = [("lt0", (R - x) % N, c) for x in range(N) for c in range(NCH)]
    per = -(-len(ltk) // (JB - 1))
    for b in range(JB):
        D("ljm%d" % b, 128 * JBW * 4, [], [("jmi", b)], T.jmi[:, JBW * b:JBW * b + JBW], T.jm[:, JBW * b:JBW * b + JBW], bonus=FIRST * (8.5 - b))
        for _, s, c in ltk[per * b:per * b + per]:
            D("llt", 16384 // NCH, [], [("lt0", s, c)], B("lt0", 64 * s + K * c, 64 * s + K * c + K), T.lt[:, NK * s + n * c:NK * s + n * c + n], bonus=FIRST * (8.0 - b))
        if b == 0:
            D("lst", 65536, [], ["sti"], T.sti[:], T.st[:], bonus=8 * FIRST)
    D("lcf", 128 * W * 2, [], [("C", 0)], T.CW[:, 0:W], T.cf[:], bonus=2 * FIRST)
    yk = [("y0l", c) for c in range(NCH)]
    V(1024, [], ["ones"], "set", T.ones[:], 1.0)
    V(1024, [], ["SM0"], "set", T.SM[:], 0.0)
    for e in range(NT):
        V(32, [], [("pad", e)], "set", T.CW[:, CWID * e + W:CWID * e + CWID], 0.0)
    add("g", 1200.0, [], ["io5"], [lambda g: g.iota(T.io5[:], [[1, 576]], 0, 0, allow_small_or_imprecise_dtypes=True)], sem="kg")
    add("g", 130.0, [], ["ipi"], [lambda g: g.iota(T.ipi[:], [[0, 2]], 0, 1)], sem="kg")
    V(2, ["ipi"], ["ipj"], "ts", T.ipj[:], T.ipi[:], 15, None, ALU.bitwise_and)
    V(2, ["ipj"], ["ipf"], "copy", T.ipf[:], T.ipj[:])
    pick("RM", T.RM[:], T.ones[:], [[-1, 16], [-16, 8], [0, 16]], ALU.is_equal, 0, 1, 2048, "ones")
    pick("b8a", T.b8a[:], T.ones[:, 0:8], [[-16, 8]], ALU.is_ge, 0, 1, 8, "ones")
    pick("b8", T.b8[:], T.b8a[:], [[16, 8]], ALU.is_ge, 15, -1, 8, "b8a")
    pick("ID", T.ID[:], T.ones[:, 0:128], [[-1, 128]], ALU.is_equal, 0, 1, 128, "ones")
    V(128, ["ID"], ["I4"], "ts", T.I4[:], T.ID[:], 18.0 * HIT / STOP, None, ALU.mult)
    V(128, ["ID"], ["I8"], "ts", T.I8[:], T.ID[:], -36.0 * HIT / STOP, None, ALU.mult)
    smk = [("SM", r) for r in range(16)]
    for r in range(16):
        V(8, ["b8", "SM0"], [("SM", r)], "ts", T.SM[:, 129 * r:128 * r + 128:16], T.b8[:], HIT, None, ALU.mult)
    pick("LTa", T.LTa[:], T.ones[:, 0:128], [[-16, 8], [0, 16]], ALU.is_ge, 0, 1, 128, "ones")
    pick("LTb", T.LTb[:], T.LTa[:], [[16, 8], [0, 16]], ALU.is_ge, 15, -1, 128, "LTa")
    pick("LTR", T.LTR[:], T.LTb[:], [[1, 128]], ALU.is_gt, 0, -1, 128, "LTb")
    for bi, be in enumerate((8, 4, 2, 1)):
        for m, (step, base) in enumerate(((1000, 0), (-1000, 1000), (1000, -be), (-1000, 1000 - be))):
            j = 4 * bi + m
            pick(("AM", j), T.AM[:, 128 * j:128 * j + 128], T.ones[:, 0:128], [[-2 * be, 64 // be], [step, 2], [-1, be]], ALU.is_equal, base, 1, 128, "ones")
    ik = [("I", b) for b in range(8)]
    for b in range(8):
        S(576, ["io5"], [("I", b)], T.JW[:, 576 * b:576 * b + 576], T.io5[:], AF.Exp, bias=float(576 * b * SC), scale=float(SC))
    jk = {0: [("J", 0, b) for b in range(JB)]}
    lk = {0: ltk}
    for b in range(JB):
        a, z = JBW * b, JBW * b + JBW
        V(JBW, [("jmi", b)], [("jmf", b)], "copy", T.jmf[:, a:z], T.jmi[:, a:z])
        S(JBW, [("jmf", b)], [("J", 0, b)], T.JW[:, W + a:W + z], T.jmf[:, a:z], AF.Exp, scale=float(SC))
    for e in range(1, NT):
        jk[e] = jk[e - 1] + [("J", e)]
        lk[e] = [("lt", e)]
        send(R - e, "rl%d" % e, 131072, ltk, ("lt", e), B("lt%d" % e, 0, 512), T.lt0[:], bonus=FIRST)
    for e in range(1, NT):
        pace = [("J", e - 1), ("C", e - 1)] if e > 1 else []
        send(R - e, "rj%d" % e, 128 * W * 2, jk[0] + pace, ("J", e), T.JW[:, W * (1 + e):W * (2 + e)], T.JW[:, W:2 * W], bonus=FIRST if e == 1 else 0.0)
        send(R - e, "rc%d" % e, 128 * W * 2, [("C", 0)] + pace, ("C", e), T.CW[:, CWID * e:CWID * e + W], T.CW[:, 0:W])
    wn = [0]

    def wbank():
        wn[0] += 1
        return "w%d" % (wn[0] % NCH)

    def smat(r):
        return T.SM[:, 128 * r:128 * r + 128]

    def rep(src, natural, reads):
        wb = wbank()
        P(["RM"] + reads, [wb], [(B(wb, K * r, K * r + K) if natural else B(wb, r, n, 16), T.RM[:, 128 * r:128 * r + 128], src, True, True, K) for r in range(16)])
        return wb

    def onehot(out, key, src, natural, reads):
        wb = rep(src, natural, reads)
        V(n, ["ipf"], [wb, key], "ts", out, B(wb, 0, n), 15.0, T.ipf[:, 0:1], ALU.min, ALU.is_equal)

    def oh_of(off, e, c):
        a = NK * OHS.index((off, e)) + n * c
        return T.oh[:, a:a + n], ("oh", off, e, c)

    def slot_letters(off, e):
        s = (R - off) % N
        return B("lt%d" % e, 64 * s, 64 * s + 64)

    def onehots(off, e):
        s = 64 * ((R - off) % N)
        for c in range(NCH):
            out, key = oh_of(off, e, c)
            onehot(out, key, B("lt%d" % e, s + K * c, s + K * c + K), False, lk[e])

    def gates(w, i, x, e, src, reads):
        es, ej = "es%d%d" % (w, i), "ej%d%d" % (w, i)
        a = 64 * x
        big = W * (1 + e) / A
        V(32, reads, [(es, x)], "ts", B(es, a, a + 64), src, 15.5, STOP, ALU.is_gt, ALU.mult)
        S(64, [(es, x)], [(ej, x)], B(ej, a, a + 64), B(es, a, a + 64), AF.Copy, bias=float(big), scale=float(-big / STOP))

    for c in range(NCH):
        onehot(B("ohn", n * c, n * c + n), ("ohn", c), B("y0l", K * c, K * c + K), True, yk)
    V(128, ["sti"], ["stu"], "copy", T.stu[:], T.sti[:])

    def image(c, lst, lkey, lo, hi, oh, ohk, tk, natural, out, okey):
        mj, ps = "mj%d" % c, "ps%d" % c
        V(1.5 * n, [lkey, ohk] + tk, [mj], "tt", B(mj, 0, n), T.JW[:, lo:hi].indirect(lst), oh, ALU.mult)
        P(smk + [mj], [ps], [(B(ps, 0, K), smat(r), B(mj, K * r, K * r + K) if natural else B(mj, r, n, 16), r == 0, r == 15, K) for r in range(16)])
        S(K, [], [ps, okey], out, B(ps, 0, K), AF.Ln, scale=float(1.0 / HIT))

    def jlist(c, t, tkey, w, i, x):
        ej, jl, ta = "ej%d%d" % (w, i), "jl%d" % c, B("ta%d" % c, 0, K)
        a = 64 * x + K * c
        V(K, [tkey, (ej, x)], [("jt", c)], "tt", ta, t, B(ej, a, a + K), ALU.add)
        V(K, [("jt", c)], [jl], "ts", B(jl, 0, K), ta, float(A), None, ALU.mult)

    def gate(c, t, tkey, w, i, x):
        es = "es%d%d" % (w, i)
        a = 64 * x + K * c
        te = B("ta%d" % c, K, 2 * K)
        V(2 * K, [tkey, (es, x)], [("te", c)], "tt", te, t, B(es, a, a + K), ALU.max)
        return te, ("te", c)

    def clist(c, te, tek, stop, skeys, touched):
        t2, cl = B("ta%d" % c, 2 * K, 3 * K), "cl%d" % c
        V(2 * K, [tek] + skeys, touched + [("t2", c)], "tt", t2, te, stop, ALU.max)
        V(K, [("t2", c)], [cl], "ts", B(cl, 0, K), t2, float(A), float(A * STOP), ALU.mult, ALU.min)

    def coefs(c, e, out, okey):
        cl = "cl%d" % c
        for q in range(NH):
            S(1.5 * h, [cl, ("C", e), ("pad", e)], [(okey, q)], B(out, h * q, h * q + h),
              T.CW[:, CWID * e:CWID * e + CWID].indirect(B(cl, K // NH * q, K // NH * (q + 1))), AF.Copy)

    state = [{} for _ in range(NCH)]

    def enter(w, i, off, c, dd):
        st = state[c]
        cur[0] = c
        if i == 0:
            oh = ("ohn", "ohy")[w]
            tt, cl, vb = "tt%d" % c, "cl%d" % c, "vb%d" % c
            image(c, B("stu", 64 * w + K * c, 64 * w + K * c + K), "stu", W, 2 * W, B(oh, n * c, n * c + n), (oh, c), jk[0], True, B(tt, 0, K), tt)
            V(K, [tt], [cl], "ts", B(cl, 0, K), B(tt, 0, K), float(A), None, ALU.mult)
            coefs(c, 0, vb, vb)
            st["t"], st["tk"] = B(tt, 0, K), tt
            st["v"], st["vk"] = vb, [(vb, q) for q in range(NH)]
            st["dead"] = None
        else:
            vi, ti, di = "vi%d%d%d" % (w, i - 1, c), "ti%d%d%d" % (w, i - 1, c), "di%d%d" % (w, i - 1)
            st["t"], st["tk"] = B(ti, 0, K), ti
            st["v"], st["vk"] = vi, [vi]
            st["dead"] = (B(di, K * c, K * c + K), (di, c))
            S(K, [(di, c)], [(dd, 0, c)], B(dd, K * c, K * c + K), B(di, K * c, K * c + K), AF.Copy)

    def lookup(w, i, off, m, c, slots, k):
        st = state[c]
        cur[0] = c
        e, x = slots[k]
        jl = "jl%d" % c
        jlist(c, st["t"], st["tk"], w, i, x)
        if w == 1 and i == 0 and k == 0:
            oh, ohk = B("ohr", n * c, n * c + n), ("ohr", c)
        else:
            oh, ohk = oh_of(off, e, c)
        hop = k + 1 == len(slots) and i + 1 < len(ST[w])
        tb = ("to%d%d%d" % (w, i, c)) if hop else ("tt%d" % c)
        image(c, B(jl, 0, K), jl, 0, W * (2 + e), oh, ohk, ik + jk[e], False, B(tb, 0, K), tb)
        st["t"], st["tk"] = B(tb, 0, K), tb
        if hop:
            ti = "ti%d%d%d" % (w, i, c)
            send(R + m, "rt%d%d%d" % (w, i, c), 128 * K * 4, [tb], ti, B(ti, 0, K), B(tb, 0, K))
        st["te"] = gate(c, st["t"], st["tk"], w, i, x)

    def station(w, i, off, m):
        slots = [(e, e + (1 if w == 1 and i == 0 else 0)) for e in range(m)]
        if w == 1 and i == 0:
            slots = [(0, 0)] + slots
        final = i + 1 == len(ST[w])
        dst = R - off if final else R + m
        dd, es = "dd%d%d" % (w, i), "es%d%d" % (w, i)
        do, di = "do%d%d" % (w, i), "di%d%d" % (w, i)
        for c in range(NCH):
            enter(w, i, off, c, dd)
        for c in range(NCH):
            lookup(w, i, off, m, c, slots, 0)
        for k, (e, x) in enumerate(slots):
            first, last = k == 0, k + 1 == len(slots)
            nat = last and final
            for c in range(NCH):
                st = state[c]
                cur[0] = c
                cl, cc, sg, ps, vo, vi = "cl%d" % c, "cc%d" % c, "sg%d" % c, "ps%d" % c, "vo%d%d%d" % (w, i, c), "vi%d%d%d" % (w, i, c)
                pv = ["pv%d%d" % (q, c) for q in range(NH)]
                te, tek = st["te"]
                if first and st["dead"] is None:
                    V(K, [tek], [cl], "ts", B(cl, 0, K), te, float(A), None, ALU.mult)
                elif first:
                    clist(c, te, tek, st["dead"][0], [st["dead"][1]], [])
                v, vk = st["v"], st["vk"]
                if not nat:
                    for q in range(NH):
                        P(["ID"] + vk, [pv[q]], [(B(pv[q], 0, h), T.ID[:], B(v, h * q, h * q + h), True, False, h)])
                coefs(c, e, cc, cc)
                for q in range(NH):
                    if not nat:
                        P(["ID", (cc, q)], [pv[q]], [(B(pv[q], 0, h), T.ID[:], B(cc, h * q, h * q + h), False, True, h)])
                    else:
                        mm = []
                        for r in range(16 // NH * q, 16 // NH * (q + 1)):
                            o = B(pv[q], K * r - h * q, K * r - h * q + K)
                            mm.append((o, T.ID[:], B(v, r, n, 16), True, False, K))
                            mm.append((o, T.ID[:], B(cc, r, n, 16), False, True, K))
                        P(["ID"] + [(cc, y) for y in range(NH)] + vk, [pv[q]], mm)
                vd = vo if last else "vb%d" % c
                for q in range(NH):
                    S(h, [], [pv[q], (sg, q)], B(sg, h * q, h * q + h), B(pv[q], 0, h), AF.Sign, bias=0.5)
                for q in range(NH):
                    V(h, [], [pv[q], (vd, q)], "ts", B(vd, h * q, h * q + h), B(pv[q], 0, h), 255.0, -255.0, ALU.min, ALU.max)
                st["v"], st["vk"] = vd, [(vd, q) for q in range(NH)]
                if last:
                    send(dst, "rv%d%d%d" % (w, i, c), 128 * n * 2, st["vk"], vi, B(vi, 0, n), B(vo, 0, n))
                else:
                    lookup(w, i, off, m, c, slots, k + 1)
                ea = 64 * x + K * c
                pk = ["I4", (es, x)]
                cnt = B(ps, K, 2 * K)
                mm = [(cnt, T.I4[:], B(es, ea, ea + K), True, False, K)]
                if st["dead"] is not None:
                    mm.append((cnt, T.I8[:], st["dead"][0], False, False, K))
                    pk += ["I8", st["dead"][1]]
                for r in range(16):
                    mm.append((cnt, smat(r), B(sg, K * r, K * r + K) if nat else B(sg, r, n, 16), False, r == 15, K))
                P(smk + pk + [(sg, q) for q in range(NH)], [ps], mm)
                a, z = 64 * (x + 1) + K * c, K * c
                if not last:
                    te, tek = st["te"]
                    clist(c, te, tek, cnt, [], [ps])
                    V(K, [], [ps, (dd, x + 1, c)], "ts", B(dd, a, a + K), cnt, -HIT, STOP, ALU.is_gt, ALU.mult)
                    st["dead"] = (B(dd, a, a + K), (dd, x + 1, c))
                else:
                    V(K, [], [ps, (do, c)], "ts", B(do, z, z + K), cnt, -HIT, STOP, ALU.is_gt, ALU.mult)
                    send(dst, "rd%d%d%d" % (w, i, c), 128 * K * 2, [(do, c)], (di, c), B(di, z, z + K), B(do, z, z + K))
                    S(K, [(do, c)], [(dd, x + 1, c)], B(dd, a, a + K), B(do, z, z + K), AF.Copy)
        cur[0] = None
        settle(w, i, off, dd, slots)

    def store_yl(s, buf, a, key):
        for c in range(NCH):
            D("stores", 16384 // NCH, [key], [("out",)], T.yl[:, NK * s + n * c:NK * s + n * c + n], B(buf, a + K * c, a + K * c + K))

    src1 = {}

    def settle(w, i, off, dd, slots):
        hi, ls = "hi%d%d" % (w, i), "ls%d%d" % (w, i)
        for e, x in slots:
            if w == 1 and i == 0 and x == 0:
                continue
            b = 64 * x
            dk = [(dd, x + 1, c) for c in range(NCH)]
            if i == 0 and x == 0:
                hit, hk = B(dd, 64, 128), dk
            else:
                V(128, dk + [(dd, x, c) for c in range(NCH)], [(hi, x)], "tt", B(hi, b, b + 64), B(dd, b + 64, b + 128), B(dd, b, b + 64), ALU.subtract)
                hit, hk = B(hi, b, b + 64), [(hi, x)]
            src, sk = (slot_letters(off, e), lk[e]) if w == 0 else src1[(i, e)]
            o = B(ls, 64 * e, 64 * e + 64)
            V(128, sk + hk, [(ls, e)], "tt", o, src, hit, ALU.max)
            if w == 1:
                V(32, [(ls, e)], [("yo", i, e)], "ts", o, o, 16.0, None, ALU.min)
                if e == 0:
                    store_yl((R - off) % N, ls, 0, ("yo", i, 0))
                else:
                    yr = "yr%d%d" % (i, e)
                    send(R + e, "ry%d%d" % (i, e), 16384, [("yo", i, e)], yr, B(yr, 0, 64), o)
                    store_yl((R - e - off) % N, yr, 0, yr)
        if w == 0:
            for a, b, lo, hh in MOVES:
                if a == i:
                    mv = "mv%d%d" % (a, b)
                    send(R - off + ST[1][b][0], "rmv%d%d" % (a, b), 16384 * (hh - lo), [(ls, d - off) for d in range(lo, hh)], mv,
                         B(mv, 0, 64 * (hh - lo)), B(ls, 64 * (lo - off), 64 * (hh - off)))

    for i, (off, m) in enumerate(ST[0]):
        for e in range(m):
            gates(0, i, e, e, slot_letters(off, e), lk[e])
    for e in range(NT):
        for q in OHS:
            if q[1] == e:
                onehots(q[0], e)
        if e == 0:
            for c in range(NCH):
                onehot(B("ohr", n * c, n * c + n), ("ohr", c), B("y0l", K * c, K * c + K), False, yk)
    for i, (off, m) in enumerate(ST[0]):
        station(0, i, off, m)
    hv, hd = "vi0%d" % (len(ST[0]) - 1), "di0%d" % (len(ST[0]) - 1)
    for c in range(NCH):
        a = K * c
        V(K, [(hd, c)], [("es10", 0)], "copy", B("es10", a, a + K), B(hd, a, a + K))
        S(K, [(hd, c)], [("ej10", 0)], B("ej10", a, a + K), B(hd, a, a + K), AF.Copy, bias=float(W / A), scale=float(-W / A / STOP))
    for b, (off, m) in enumerate(ST[1]):
        for e in range(m):
            d = off + e
            for a, (o0, m0) in enumerate(ST[0]):
                if o0 <= d < o0 + m0:
                    if o0 == off:
                        ap, key = B("ls0%d" % a, 64 * (d - o0), 64 * (d - o0) + 64), [("ls0%d" % a, d - o0)]
                    else:
                        lo = max(o0, off)
                        ap, key = B("mv%d%d" % (a, b), 64 * (d - lo), 64 * (d - lo) + 64), ["mv%d%d" % (a, b)]
            src1[(b, e)] = (ap, key)
            gates(1, b, e + (1 if b == 0 else 0), e, ap, key)
    for c in range(NCH):
        vi = hv + str(c)
        ax, am = "ax%d" % c, "am%d" % c
        src, sk, wd, pos = vi, vi, n, 0
        for bi in range(4):
            hf = wd // 2
            wb = wbank()
            mm = []
            for j in range(2):
                for k in range(2):
                    q = 4 * bi + 2 * j + k
                    mm.append((B(wb, hf * j, hf * j + hf), T.AM[:, 128 * q:128 * q + 128], B(src, pos + hf * k, pos + hf * k + hf), k == 0, k == 1, hf))
            P([("AM", 4 * bi + y) for y in range(4)] + [sk], [wb], mm)
            S(hf, [], [wb, ax], B(ax, 0, hf), B(wb, 0, hf), AF.Copy)
            npos = 0 if bi == 0 else pos + wd
            V(hf, [ax], [wb, (am, bi)], "tt", B(am, npos, npos + hf), B(ax, 0, hf), B(wb, hf, 2 * hf), ALU.max)
            src, sk, wd, pos = am, (am, bi), hf, npos
        wb = rep(B(am, pos, pos + K), True, [(am, 3)])
        V(n, [vi], [wb, (am, "eq")], "tt", B(am, n, 2 * n), B(vi, 0, n), B(wb, 0, n), ALU.is_equal)
        w2 = wbank()
        P(["LTR", (am, "eq")], [w2], [(B(w2, 0, n), T.LTR[:], B(am, n, 2 * n), True, True, n)])
        V(n, [(am, "eq")], [w2, ("ohy", c)], "tt", B("ohy", n * c, n * c + n), B(am, n, 2 * n), B(w2, 0, n), ALU.is_gt)
    for i, (off, m) in enumerate(ST[1]):
        station(1, i, off, m)
    for c in range(NCH):
        ax, d1, v1 = "ax%d" % c, "di1%d" % (len(ST[1]) - 1), "vi1%d%d" % (len(ST[1]) - 1, c)
        a = K * c
        S(n, [("ohy", c), "ipf"], [ax], B(ax, 0, n), B("ohy", n * c, n * c + n), AF.Copy, scale=T.ipf[:, 0:1])
        wb = wbank()
        P(smk + [ax], [wb], [(B(wb, 0, K), smat(r), B(ax, K * r, K * r + K), r == 0, r == 15, K) for r in range(16)])
        y1, ym = B("y1l", a, a + K), B("yim", a, a + K)
        V(K, [], [wb, ("y1l", c)], "ts", y1, B(wb, 0, K), float(1.0 / HIT), None, ALU.mult)
        V(K, [("y0l", c), (hd, c)], [("yim", c)], "tt", ym, B("y0l", a, a + K), B(hd, a, a + K), ALU.max)
        V(K, [("yim", c), ("dd10", 1, c)], [("yiu", c)], "tt", ym, ym, B("dd10", 64 + a, 64 + a + K), ALU.max)
        V(K, [("yiu", c)], [("yi0", c)], "ts", B("yit", a, a + K), ym, 16.0, None, ALU.min)
        V(K, [("y1l", c), (d1, c)], [("y1m", c)], "tt", y1, y1, B(d1, a, a + K), ALU.max)
        V(K, [("y1m", c)], [("yi1", c)], "ts", B("yit", 64 + a, 64 + a + K), y1, 16.0, None, ALU.min)
        for t in range(2):
            D("stores", 16384 // NCH, [("yi%d" % t, c)], [("out",)], T.yi[:, NK * t + n * c:NK * t + n * c + n], B("yit", 64 * t + a, 64 * t + a + K))
        D("stores", 128 * n * 2, [v1], [("out",)], T.yv[:, n * c:n * c + n], B(v1, 0, n))
    return ops


def depend(ops):
    writer, readers = {}, {}
    for k, o in enumerate(ops):
        d = {}
        for key in o["r"]:
            for x in writer.get(key, []):
                d[x] = True
        for key in o["w"]:
            if key == ("out",):
                continue
            for x in writer.get(key, []) + readers.get(key, []):
                d.setdefault(x, False)
        if "after" in o:
            d[o["after"]] = True
        o["d"] = d
        for key in o["w"]:
            if key in (("es10", 0), ("ej10", 0)):
                writer.setdefault(key, []).append(k)
            else:
                writer[key] = [k]
            readers[key] = []
        for key in o["r"]:
            readers.setdefault(key, []).append(k)


def kind(o):
    name = o["w"][-1] if o["w"] else (o["r"][0] if o["r"] else "")
    name = (name if isinstance(name, str) else name[0]).rstrip("0123456789")
    return name + ("c" if o["q"] == "pe" and any(str(x[0]).startswith("sg") for x in o["r"]) else "")


def order(ops):
    cnt = len(ops)
    nxt = [[] for _ in range(cnt)]
    for k, o in enumerate(ops):
        for x in o["d"]:
            nxt[x].append(k)
    prio = [0.0] * cnt
    for k in range(cnt - 1, -1, -1):
        o = ops[k]
        best = 0.0
        for y in nxt[k]:
            best = max(best, prio[y] + WAKE)
        prio[k] = best + o["dur"] + o["lat"] + o["tail"]
    urge = [prio[k] + o["bonus"] + URGE[o["ch"]].get(kind(o), 0) for k, o in enumerate(ops)]
    left = [len(o["d"]) for o in ops]
    ready = [0.0] * cnt
    cand = {}
    for k in range(cnt):
        if left[k] == 0:
            cand.setdefault(ops[k]["q"], []).append(k)
    free, lane, out = {}, 0.0, []

    def rank(x):
        return urge[x]
    while cand:
        t, q = None, None
        for y in cand:
            f = max(free.get(y, 0.0) if y != "net" else 0.0, min(ready[k] for k in cand[y]))
            if t is None or f < t:
                t, q = f, y
        k = max((x for x in cand[q] if ready[x] <= t + (GAP if q != "net" else 0.0)), key=rank)
        if ready[k] > t:
            fit = [x for x in cand[q] if ready[x] <= t and t + ops[x]["dur"] <= ready[k] + 20.0]
            if fit:
                k = max(fit, key=rank)
            else:
                t = ready[k]
        cand[q].remove(k)
        if not cand[q]:
            del cand[q]
        o = ops[k]
        end = t + o["dur"]
        free[q] = end
        if o["tail"]:
            lane = max(end, lane) + o["tail"]
            end = lane + o["lat"]
        out.append(k)
        for y in nxt[k]:
            left[y] -= 1
            ready[y] = max(ready[y], end + (WAKE if ops[y]["q"] != q else SELF))
            if left[y] == 0:
                cand.setdefault(ops[y]["q"], []).append(y)
    return out


QSEM = {"pe": "kpe", "v": "kv", "s": "ks"}


def rank_program(g, core, T, topo):
    rank = T.rank_of(core)
    if rank is None:
        return
    ops = program(rank, T, topo)
    depend(ops)
    seq = order(ops)
    total = {}
    for o in ops:
        if o["dma"]:
            total[o["sem"]] = total.get(o["sem"], 0) + 16
    eng = {"pe": g.tensor, "v": g.vector, "s": g.scalar, "g": g, "sync": g.sync}
    count, sent, arrived, know = {}, 0, {}, {}
    for k in seq:
        o = ops[k]
        q = o["q"]
        if q == "net":
            o["done"] = [(o["sem"], o["cnt"])]
            o["know"] = {o["sem"]: o["cnt"]}
            arrived[o["sem"]] = o["cnt"]
            continue
        mine = know.setdefault(q, {})
        need, merge = {}, []
        for x, hard in o["d"].items():
            p = ops[x]
            if p["sem"] == "remote" or (not hard and p["q"] == q == "pe"):
                continue
            for s, c in p["done"]:
                if mine.get(s, 0) < c:
                    need[s] = max(need.get(s, 0), c)
            merge.append(x)
        for s in sorted(need):
            implied = False
            for x in merge:
                if ops[x]["know"].get(s, 0) >= need[s] and ops[x]["done"][0][0] != s:
                    implied = True
            if not implied:
                eng[q].wait_ge(T.sem[s], int(need[s]))
        for x in merge:
            for s, c in ops[x]["know"].items():
                mine[s] = max(mine.get(s, 0), c)
        sem = o["sem"] or QSEM.get(q)
        for call in o["calls"]:
            ins = call(g)
            if sem == "remote":
                sent += o["cnt"]
            elif o["dma"]:
                ins.then_inc(T.sem[sem], 16)
            else:
                count[sem] = count.get(sem, 0) + 1
                ins.then_inc(T.sem[sem], 1)
        o["know"] = dict(mine)
        if sem == "remote":
            o["done"] = []
            continue
        c = total[sem] if o["dma"] else count[sem]
        o["done"] = [(sem, c)]
        o["know"][sem] = max(o["know"].get(sem, 0), c)
    for s in ("kpe", "kv", "ks", "kg"):
        g.wait_ge(T.sem[s], int(count[s]))
    for s in sorted(total):
        g.wait_ge(T.sem[s], int(total[s]))
    for s in sorted(arrived):
        g.wait_ge(T.sem[s], int(arrived[s]))
    g.wait_ge(T.sem.ls, int(sent))
